import numpy as np, ml_dtypes
CORES = [56,61,80,85]
N = 4
import mx_ref
NC, G, MB = 128, 2, 3
C = np.float32(0.037)
BF = ml_dtypes.bfloat16
def cut(t, i, w=512):
    return t[:, w * i:w * i + w]
def tile(rs):
    return np.stack(rs, axis=2).reshape(128, -1).astype(BF)
def layer(w, X):
    out = []
    for i in range(G):
        for t in range(len(X)):
            p = mx_ref.matmul(mx_ref.quantize(cut(w, len(X) * i + t)), X[t])
            z = p if t == 0 else z + p
        out.append(z)
    return out
def act(Z):
    return [np.maximum(s * z, 0) * C for z in Z for s in (1, -1)]
def setup_inputs(rng):
    def f(*shape):
        return mx_ref.flush((rng.standard_normal(shape, dtype=np.float32) * np.exp2(rng.integers(-2, 3, shape[:-1] + (1,)))).astype(BF))
    return {"x": f(N, 128, MB * 4 * NC), "w": f(N, 128, G * 512)}
def setup_inputs_blocks(rng):
    d = setup_inputs(rng)
    for k in ("x",): d[k] = mx_ref.spread(d[k], rng, 4)
    for k in ("w",): d[k] = mx_ref.spread(d[k], rng, 1)
    return d
def setup_inputs_wide(rng):
    d = setup_inputs(rng)
    for k in ("x",): d[k] = mx_ref.flush((d[k].astype(np.float32) * np.exp2(rng.integers(-8, 9, (N, 1, 1))).astype(np.float32)).astype(BF))
    return d
def setup_inputs_zeros(rng):
    d = setup_inputs(rng); v = d["x"].reshape(N, 128, -1, 4).copy()
    v[np.broadcast_to((rng.random((N, 1, v.shape[2], 1)) < 0.33), v.shape)] = 0
    d["x"] = v.reshape(d["x"].shape)
    return d
def reference(x, w):
    y = np.full((N, 128, MB * G * NC), np.nan, np.float32)
    for m in range(MB):
        a = mx_ref.quantize(cut(x[N - 1], m, 4 * NC))
        for s in range(N - 1):
            a = mx_ref.quantize(tile(act(layer(w[s], [a]))))
        Z = layer(w[N - 1], [a])
        for i in range(G):
            y[N - 1][:, NC * (G * m + i):NC * (G * m + i) + NC] = Z[i]
    return {"y": y}

@@ -1,0 +1,140 @@
+from concourse.mybir import dt, AluOpType, ActivationFunctionType
+
+SIM_CORES = 96
+NT, NC, G = 3, 128, 2
+C = 0.037
+CHUNKS = [(0, 1), (1, 2), (2, 3)]
+K_ON, K_OFF = 8, 8
+
+SCRATCH = {
+    "xb": ("sbuf", [128, NT * 4 * NC], "bfloat16"),
+    "wb": ("sbuf", [128, G * 512], "bfloat16"),
+    "wcod": ("sbuf", [128, G * 128], "float8_e4m3fn_x4"),
+    "wscl": ("sbuf", [128, G * 128], "uint8"),
+    "icod": ("sbuf", [128, NT * NC], "float8_e4m3fn_x4"),
+    "iscl": ("sbuf", [128, NT * NC], "uint8"),
+    "ocod": ("sbuf", [128, NT * NC], "float8_e4m3fn_x4"),
+    "oscl": ("sbuf", [128, NT * NC], "uint8"),
+    "h": ("sbuf", [128, NT * 4 * NC], "bfloat16"),
+    "yb": ("sbuf", [128, NT * G * NC], "float32"),
+    "ps": ("psum", [128, 512 * G * len(CHUNKS)], "float32"),
+}
+SEMAPHORES = (["wl", "wq", "yd", "sent"]
+              + [n + str(j) for j in range(len(CHUNKS)) for n in ("xl", "q", "a", "za", "zb", "h", "yc")])
+
+
+def _engines(topo, src, dst):
+    full = topo.mask(src, dst)
+    bits = [b for b in range(full.bit_length()) if (full >> b) & 1]
+    k = min(K_ON if topo.chip(src) == topo.chip(dst) else K_OFF, len(bits))
+    m = 0
+    for b in bits[::len(bits) // k][:k]:
+        m |= 1 << b
+    return m, k
+
+
+def _writes(T, topo):
+    cores = list(T.cores)
+    chain = [cores[-1]] + cores
+    out = []
+    for src, dst in zip(chain, chain[1:]):
+        if topo.may_write(src, dst):
+            paths = [[src, dst], [src, dst]]
+        else:
+            own = [c for c in range(SIM_CORES) if topo.chip(c) == topo.chip(src) and T.rank_of(c) is None
+                   and topo.may_write(c, dst)]
+            near = [c for c in own if topo.die(c) == topo.die(src)]
+            far = [c for c in own if topo.die(c) != topo.die(src)]
+            paths = [[src, (near + far)[0], dst], [src, (far + near[1:] + near)[0], dst]]
+        for kind, p in enumerate(paths):
+            for i in range(len(p) - 1):
+                out.append((p[i], p[i + 1], kind, i == 0))
+    return out
+
+
+def rank_program(g, core, T, topo):
+    writes = _writes(T, topo)
+    outgoing = [w for w in writes if w[0] == core]
+    incoming = [w for w in writes if w[1] == core]
+    if not outgoing and not incoming:
+        return
+    S = T.sem
+    need = sum(_engines(topo, w[0], w[1])[1] for w in incoming)
+    rank = T.rank_of(core)
+    last = len(T.cores) - 1
+
+    def send(j):
+        a, b = CHUNKS[j][0] * NC, CHUNKS[j][1] * NC
+        for (_, dst, kind, fresh) in outgoing:
+            rid, pid, _se = topo.addr(dst)
+            mask, _k = _engines(topo, core, dst)
+            if kind == 0:
+                src_ap = (T.ocod if fresh else T.icod)[:, a:b].bitcast(dt.uint8)
+                dst_ap = T.icod[:, a:b].bitcast(dt.uint8)
+            else:
+                src_ap = (T.oscl if fresh else T.iscl)[:, a:b]
+                dst_ap = T.iscl[:, a:b]
+            g.remote_dma(out_ap=dst_ap, in_ap=src_ap, remote_sem=S["a%d" % j], local_sem=S.sent,
+                         pid=pid, routing_id=rid, dma_engine_mask=mask)
+
+    all_sent = len(CHUNKS) * sum(_engines(topo, core, w[1])[1] for w in outgoing)
+
+    if rank is None:
+        for j in range(len(CHUNKS)):
+            g.wait_ge(S["a%d" % j], need)
+            send(j)
+        g.wait_ge(S.sent, all_sent)
+        return
+
+    if rank == last:
+        for j, (t0, t1) in enumerate(CHUNKS):
+            g.sync.dma_start(T.xb[:, 512 * t0:512 * t1], T.x[:, 512 * t0:512 * t1]).then_inc(S["xl%d" % j], 16)
+    g.sync.dma_start(T.wb[:], T.w[:]).then_inc(S.wl, 16)
+    if rank == last:
+        for j, (t0, t1) in enumerate(CHUNKS):
+            g.vector.wait_ge(S["xl%d" % j], 16)
+            g.vector.quantize_mx(T.ocod[:, NC * t0:NC * t1], T.oscl[:, NC * t0:NC * t1],
+                                 T.xb[:, 512 * t0:512 * t1]).then_inc(S["q%d" % j], 1)
+            g.wait_ge(S["q%d" % j], 1)
+            send(j)
+    g.vector.wait_ge(S.wl, 16)
+    g.vector.quantize_mx(T.wcod[:], T.wscl[:], T.wb[:]).then_inc(S.wq, 1)
+    g.tensor.wait_ge(S.wq, 1)
+
+    for j, (t0, t1) in enumerate(CHUNKS):
+        n = NC * (t1 - t0)
+        g.tensor.wait_ge(S["a%d" % j], need)
+        z = []
+        for i in range(G):
+            bank = 512 * (G * j + i)
+            z.append(bank)
+            g.tensor.matmul_mx(T.ps[:, bank:bank + n], T.wcod[:, 128 * i:128 * i + 128],
+                               T.wscl[:, 128 * i:128 * i + 128], T.icod[:, NC * t0:NC * t1],
+                               T.iscl[:, NC * t0:NC * t1], True, True).then_inc(S[("za%d", "zb%d")[i] % j], 1)
+        if rank != last:
+            lo, hi = 512 * t0, 512 * t1
+            z0, z1 = T.ps[:, z[0]:z[0] + n], T.ps[:, z[1]:z[1] + n]
+            g.scalar.wait_ge(S["za%d" % j], 1)
+            g.scalar.activation(T.h[:, lo + 0:hi:4], z0, ActivationFunctionType.Relu, scale=C).then_inc(S["h%d" % j], 1)
+            g.scalar.activation(T.h[:, lo + 1:hi:4], z0, ActivationFunctionType.Relu, scale=-C).then_inc(S["h%d" % j], 1)
+            g.vector.wait_ge(S["zb%d" % j], 1)
+            g.vector.tensor_scalar(T.h[:, lo + 2:hi:4], z1, 0.0, C, AluOpType.max, AluOpType.mult).then_inc(S["h%d" % j], 1)
+            g.vector.tensor_scalar(T.h[:, lo + 3:hi:4], z1, -C, 0.0, AluOpType.mult, AluOpType.max).then_inc(S["h%d" % j], 1)
+            g.vector.wait_ge(S["h%d" % j], 4)
+            g.vector.quantize_mx(T.ocod[:, NC * t0:NC * t1], T.oscl[:, NC * t0:NC * t1],
+                                 T.h[:, lo:hi]).then_inc(S["q%d" % j], 1)
+            g.wait_ge(S["q%d" % j], 1)
+            send(j)
+        else:
+            g.vector.wait_ge(S["za%d" % j], 1)
+            g.scalar.wait_ge(S["zb%d" % j], 1)
+            for t in range(t1 - t0):
+                c0 = NC * G * (t0 + t)
+                g.vector.tensor_copy(T.yb[:, c0:c0 + NC], T.ps[:, z[0] + NC * t:z[0] + NC * t + NC]).then_inc(S["yc%d" % j], 1)
+                g.scalar.activation(T.yb[:, c0 + NC:c0 + 2 * NC], T.ps[:, z[1] + NC * t:z[1] + NC * t + NC],
+                                    ActivationFunctionType.Copy).then_inc(S["yc%d" % j], 1)
+            g.sync.wait_ge(S["yc%d" % j], 2 * (t1 - t0))
+            g.sync.dma_start(T.y[:, NC * G * t0:NC * G * t1], T.yb[:, NC * G * t0:NC * G * t1]).then_inc(S.yd, 16)
+    if rank == last:
+        g.sync.wait_ge(S.yd, 16 * len(CHUNKS))
+    g.wait_ge(S.sent, all_sent)

@@ -2,25 +2,31 @@ from concourse.mybir import dt, AluOpType, ActivationFunctionType
 
 SIM_CORES = 96
 NT, NC, G = 3, 128, 2
+NW = NT * NC
 C = 0.037
-CHUNKS = [(0, 1), (1, 2), (2, 3)]
-K_ON, K_OFF = 8, 8
+HALF = [(0, NW // 2), (NW // 2, NW)]
+K_ON, K_OFF = 16, 8
 
 SCRATCH = {
-    "xb": ("sbuf", [128, NT * 4 * NC], "bfloat16"),
+    "xb": ("sbuf", [128, 4 * NW], "bfloat16"),
     "wb": ("sbuf", [128, G * 512], "bfloat16"),
     "wcod": ("sbuf", [128, G * 128], "float8_e4m3fn_x4"),
     "wscl": ("sbuf", [128, G * 128], "uint8"),
-    "icod": ("sbuf", [128, NT * NC], "float8_e4m3fn_x4"),
-    "iscl": ("sbuf", [128, NT * NC], "uint8"),
-    "ocod": ("sbuf", [128, NT * NC], "float8_e4m3fn_x4"),
-    "oscl": ("sbuf", [128, NT * NC], "uint8"),
-    "h": ("sbuf", [128, NT * 4 * NC], "bfloat16"),
+    "vcod": ("sbuf", [128, G * 128], "float8_e4m3fn_x4"),
+    "vscl": ("sbuf", [128, G * 128], "uint8"),
+    "icod": ("sbuf", [128, NW], "float8_e4m3fn_x4"),
+    "iscl": ("sbuf", [128, NW], "uint8"),
+    "mcod": ("sbuf", [128, NW], "float8_e4m3fn_x4"),
+    "mscl": ("sbuf", [128, NW], "uint8"),
+    "ocod": ("sbuf", [128, NW], "float8_e4m3fn_x4"),
+    "oscl": ("sbuf", [128, NW], "uint8"),
+    "h": ("sbuf", [128, 4 * NW], "bfloat16"),
+    "h2": ("sbuf", [128, 4 * NW], "bfloat16"),
     "yb": ("sbuf", [128, NT * G * NC], "float32"),
-    "ps": ("psum", [128, 512 * G * len(CHUNKS)], "float32"),
+    "ps": ("psum", [128, 512 * G * 2], "float32"),
 }
-SEMAPHORES = (["wl", "wq", "yd", "sent"]
-              + [n + str(j) for j in range(len(CHUNKS)) for n in ("xl", "q", "a", "za", "zb", "h", "yc")])
+SEMAPHORES = (["wl", "wq", "wa", "yd", "sent"]
+              + [n + str(k) for k in range(2) for n in ("xl", "xq", "a", "za", "zb", "h", "q", "yc")])
 
 
 def _engines(topo, src, dst):
@@ -35,20 +41,30 @@ def _engines(topo, src, dst):
 
 def _writes(T, topo):
     cores = list(T.cores)
-    chain = [cores[-1]] + cores
+    last = cores[-1]
+    used = set()
     out = []
-    for src, dst in zip(chain, chain[1:]):
+
+    def hop(src, dst, j):
         if topo.may_write(src, dst):
-            paths = [[src, dst], [src, dst]]
+            vias = [None, None]
         else:
-            own = [c for c in range(SIM_CORES) if topo.chip(c) == topo.chip(src) and T.rank_of(c) is None
-                   and topo.may_write(c, dst)]
-            near = [c for c in own if topo.die(c) == topo.die(src)]
-            far = [c for c in own if topo.die(c) != topo.die(src)]
-            paths = [[src, (near + far)[0], dst], [src, (far + near[1:] + near)[0], dst]]
-        for kind, p in enumerate(paths):
-            for i in range(len(p) - 1):
-                out.append((p[i], p[i + 1], kind, i == 0))
+            pool = [c for c in range(SIM_CORES) if topo.chip(c) == topo.chip(src) and T.rank_of(c) is None
+                    and c not in used and topo.may_write(c, dst)]
+            pool.sort(key=lambda c: topo.die(c) != topo.die(dst))
+            vias = (pool * 2)[:2]
+            used.update(vias)
+        for kind, v in enumerate(vias):
+            if v is None:
+                out.append((src, dst, kind, j, True))
+            else:
+                out.append((src, v, kind, j, True))
+                out.append((v, dst, kind, j, False))
+
+    for j in range(2):
+        hop(last, cores[j], j)
+        hop(cores[j], cores[2], j)
+        hop(cores[2], last, j)
     return out
 
 
@@ -59,82 +75,123 @@ def rank_program(g, core, T, topo):
     if not outgoing and not incoming:
         return
     S = T.sem
-    need = sum(_engines(topo, w[0], w[1])[1] for w in incoming)
+    cores = list(T.cores)
     rank = T.rank_of(core)
-    last = len(T.cores) - 1
+    last = len(cores) - 1
+    need = [sum(_engines(topo, w[0], w[1])[1] for w in incoming if w[3] == j) for j in range(2)]
+    sent = [0]
+
+    def put(dst, dst_ap, src_ap, sem):
+        rid, pid, _se = topo.addr(dst)
+        mask, k = _engines(topo, core, dst)
+        g.remote_dma(out_ap=dst_ap, in_ap=src_ap, remote_sem=sem, local_sem=S.sent,
+                     pid=pid, routing_id=rid, dma_engine_mask=mask)
+        sent[0] += k
 
     def send(j):
-        a, b = CHUNKS[j][0] * NC, CHUNKS[j][1] * NC
-        for (_, dst, kind, fresh) in outgoing:
-            rid, pid, _se = topo.addr(dst)
-            mask, _k = _engines(topo, core, dst)
+        a, b = HALF[j]
+        for (_, dst, kind, jj, fresh) in outgoing:
+            if jj != j:
+                continue
             if kind == 0:
-                src_ap = (T.ocod if fresh else T.icod)[:, a:b].bitcast(dt.uint8)
-                dst_ap = T.icod[:, a:b].bitcast(dt.uint8)
+                put(dst, T.icod[:, a:b].bitcast(dt.uint8), (T.ocod if fresh else T.icod)[:, a:b].bitcast(dt.uint8),
+                    S["a%d" % j])
             else:
-                src_ap = (T.oscl if fresh else T.iscl)[:, a:b]
-                dst_ap = T.iscl[:, a:b]
-            g.remote_dma(out_ap=dst_ap, in_ap=src_ap, remote_sem=S["a%d" % j], local_sem=S.sent,
-                         pid=pid, routing_id=rid, dma_engine_mask=mask)
-
-    all_sent = len(CHUNKS) * sum(_engines(topo, core, w[1])[1] for w in outgoing)
+                put(dst, T.iscl[:, a:b], (T.oscl if fresh else T.iscl)[:, a:b], S["a%d" % j])
 
     if rank is None:
-        for j in range(len(CHUNKS)):
-            g.wait_ge(S["a%d" % j], need)
-            send(j)
-        g.wait_ge(S.sent, all_sent)
+        for j in range(2):
+            if need[j]:
+                g.wait_ge(S["a%d" % j], need[j])
+                send(j)
+        g.wait_ge(S.sent, sent[0])
         return
 
+    def products(k, wc, ws, rc, rs, a, b):
+        z = []
+        for i in range(G):
+            bank = 512 * (G * k + i)
+            z.append(T.ps[:, bank:bank + b - a])
+            g.tensor.matmul_mx(z[i], wc[:, 128 * i:128 * i + 128], ws[:, 128 * i:128 * i + 128],
+                               rc[:, a:b], rs[:, a:b], True, True).then_inc(S[("za%d", "zb%d")[i] % k], 1)
+        return z
+
+    def layer(k, wc, ws, rc, rs, a, b, hb, oc, osc):
+        z0, z1 = products(k, wc, ws, rc, rs, a, b)
+        lo, hi = 4 * a, 4 * b
+        hs = S["h%d" % k]
+        g.scalar.wait_ge(S["za%d" % k], 1)
+        g.scalar.activation(hb[:, lo + 0:hi:4], z0, ActivationFunctionType.Relu, scale=C).then_inc(hs, 1)
+        g.scalar.activation(hb[:, lo + 1:hi:4], z0, ActivationFunctionType.Relu, scale=-C).then_inc(hs, 1)
+        g.vector.wait_ge(S["zb%d" % k], 1)
+        g.vector.tensor_scalar(hb[:, lo + 2:hi:4], z1, 0.0, C, AluOpType.max, AluOpType.mult).then_inc(hs, 1)
+        g.vector.tensor_scalar(hb[:, lo + 3:hi:4], z1, -C, 0.0, AluOpType.mult, AluOpType.max).then_inc(hs, 1)
+        g.vector.wait_ge(hs, 4)
+        g.vector.quantize_mx(oc[:, a:b], osc[:, a:b], hb[:, lo:hi]).then_inc(S["q%d" % k], 1)
+
     if rank == last:
-        for j, (t0, t1) in enumerate(CHUNKS):
-            g.sync.dma_start(T.xb[:, 512 * t0:512 * t1], T.x[:, 512 * t0:512 * t1]).then_inc(S["xl%d" % j], 16)
+        for j, (a, b) in enumerate(HALF):
+            g.sync.dma_start(T.xb[:, 4 * a:4 * b], T.x[:, 4 * a:4 * b]).then_inc(S["xl%d" % j], 16)
     g.sync.dma_start(T.wb[:], T.w[:]).then_inc(S.wl, 16)
     if rank == last:
-        for j, (t0, t1) in enumerate(CHUNKS):
+        for j, (a, b) in enumerate(HALF):
             g.vector.wait_ge(S["xl%d" % j], 16)
-            g.vector.quantize_mx(T.ocod[:, NC * t0:NC * t1], T.oscl[:, NC * t0:NC * t1],
-                                 T.xb[:, 512 * t0:512 * t1]).then_inc(S["q%d" % j], 1)
-            g.wait_ge(S["q%d" % j], 1)
+            g.vector.quantize_mx(T.ocod[:, a:b], T.oscl[:, a:b], T.xb[:, 4 * a:4 * b]).then_inc(S["xq%d" % j], 1)
+            g.wait_ge(S["xq%d" % j], 1)
             send(j)
     g.vector.wait_ge(S.wl, 16)
     g.vector.quantize_mx(T.wcod[:], T.wscl[:], T.wb[:]).then_inc(S.wq, 1)
-    g.tensor.wait_ge(S.wq, 1)
 
-    for j, (t0, t1) in enumerate(CHUNKS):
-        n = NC * (t1 - t0)
-        g.tensor.wait_ge(S["a%d" % j], need)
-        z = []
-        for i in range(G):
-            bank = 512 * (G * j + i)
-            z.append(bank)
-            g.tensor.matmul_mx(T.ps[:, bank:bank + n], T.wcod[:, 128 * i:128 * i + 128],
-                               T.wscl[:, 128 * i:128 * i + 128], T.icod[:, NC * t0:NC * t1],
-                               T.iscl[:, NC * t0:NC * t1], True, True).then_inc(S[("za%d", "zb%d")[i] % j], 1)
-        if rank != last:
-            lo, hi = 512 * t0, 512 * t1
-            z0, z1 = T.ps[:, z[0]:z[0] + n], T.ps[:, z[1]:z[1] + n]
-            g.scalar.wait_ge(S["za%d" % j], 1)
-            g.scalar.activation(T.h[:, lo + 0:hi:4], z0, ActivationFunctionType.Relu, scale=C).then_inc(S["h%d" % j], 1)
-            g.scalar.activation(T.h[:, lo + 1:hi:4], z0, ActivationFunctionType.Relu, scale=-C).then_inc(S["h%d" % j], 1)
-            g.vector.wait_ge(S["zb%d" % j], 1)
-            g.vector.tensor_scalar(T.h[:, lo + 2:hi:4], z1, 0.0, C, AluOpType.max, AluOpType.mult).then_inc(S["h%d" % j], 1)
-            g.vector.tensor_scalar(T.h[:, lo + 3:hi:4], z1, -C, 0.0, AluOpType.mult, AluOpType.max).then_inc(S["h%d" % j], 1)
-            g.vector.wait_ge(S["h%d" % j], 4)
-            g.vector.quantize_mx(T.ocod[:, NC * t0:NC * t1], T.oscl[:, NC * t0:NC * t1],
-                                 T.h[:, lo:hi]).then_inc(S["q%d" % j], 1)
+    if rank < 2:
+        other = cores[1 - rank]
+        g.wait_ge(S.wq, 1)
+        put(other, T.vcod[:].bitcast(dt.uint8), T.wcod[:].bitcast(dt.uint8), S.wa)
+        put(other, T.vscl[:], T.wscl[:], S.wa)
+        w_in = 2 * _engines(topo, other, core)[1]
+        a, b = HALF[rank]
+        for k in range(2):
+            if k == rank:
+                g.tensor.wait_ge(S.wq, 1)
+                wc, ws = T.wcod, T.wscl
+            else:
+                g.tensor.wait_ge(S.wa, w_in)
+                wc, ws = T.vcod, T.vscl
+            if k == 0:
+                g.tensor.wait_ge(S["a%d" % rank], need[rank])
+                layer(0, wc, ws, T.icod, T.iscl, a, b, T.h, T.mcod, T.mscl)
+            else:
+                g.tensor.wait_ge(S.q0, 1)
+                layer(1, wc, ws, T.mcod, T.mscl, a, b, T.h2, T.ocod, T.oscl)
+        g.wait_ge(S.q1, 1)
+        send(rank)
+    elif rank != last:
+        g.tensor.wait_ge(S.wq, 1)
+        for j, (a, b) in enumerate(HALF):
+            g.tensor.wait_ge(S["a%d" % j], need[j])
+            layer(j, T.wcod, T.wscl, T.icod, T.iscl, a, b, T.h, T.ocod, T.oscl)
             g.wait_ge(S["q%d" % j], 1)
             send(j)
-        else:
+    else:
+        g.tensor.wait_ge(S.wq, 1)
+        stored = 0
+        for j, (a, b) in enumerate(HALF):
+            g.tensor.wait_ge(S["a%d" % j], need[j])
+            products(j, T.wcod, T.wscl, T.icod, T.iscl, a, b)
             g.vector.wait_ge(S["za%d" % j], 1)
             g.scalar.wait_ge(S["zb%d" % j], 1)
-            for t in range(t1 - t0):
-                c0 = NC * G * (t0 + t)
-                g.vector.tensor_copy(T.yb[:, c0:c0 + NC], T.ps[:, z[0] + NC * t:z[0] + NC * t + NC]).then_inc(S["yc%d" % j], 1)
-                g.scalar.activation(T.yb[:, c0 + NC:c0 + 2 * NC], T.ps[:, z[1] + NC * t:z[1] + NC * t + NC],
+            n = 0
+            for m in range(a // NC, (b - 1) // NC + 1):
+                lo, hi = max(a, NC * m), min(b, NC * m + NC)
+                c0 = NC * G * m + lo - NC * m
+                p0 = 512 * G * j + lo - a
+                g.vector.tensor_copy(T.yb[:, c0:c0 + hi - lo], T.ps[:, p0:p0 + hi - lo]).then_inc(S["yc%d" % j], 1)
+                g.scalar.activation(T.yb[:, c0 + NC:c0 + NC + hi - lo], T.ps[:, p0 + 512:p0 + 512 + hi - lo],
                                     ActivationFunctionType.Copy).then_inc(S["yc%d" % j], 1)
-            g.sync.wait_ge(S["yc%d" % j], 2 * (t1 - t0))
-            g.sync.dma_start(T.y[:, NC * G * t0:NC * G * t1], T.yb[:, NC * G * t0:NC * G * t1]).then_inc(S.yd, 16)
-    if rank == last:
-        g.sync.wait_ge(S.yd, 16 * len(CHUNKS))
-    g.wait_ge(S.sent, all_sent)
+                n += 2
+            g.sync.wait_ge(S["yc%d" % j], n)
+            whole = b // NC
+            g.sync.dma_start(T.y[:, NC * G * stored:NC * G * whole],
+                             T.yb[:, NC * G * stored:NC * G * whole]).then_inc(S.yd, 16)
+            stored = whole
+        g.sync.wait_ge(S.yd, 16 * len(HALF))
+    g.wait_ge(S.sent, sent[0])

@@ -1,3 +1,4 @@
+from concourse.bass import DstId, RemoteDMATransfer
 from concourse.mybir import dt, AluOpType, ActivationFunctionType
 
 SIM_CORES = 96
@@ -5,7 +6,6 @@ NT, NC, G = 3, 128, 2
 NW = NT * NC
 C = 0.037
 HALF = [(0, NW // 2), (NW // 2, NW)]
-K_ON, K_OFF = 16, 8
 
 SCRATCH = {
     "xb": ("sbuf", [128, 4 * NW], "bfloat16"),
@@ -29,56 +29,78 @@ SEMAPHORES = (["wl", "wq", "wa", "yd", "sent"]
               + [n + str(k) for k in range(2) for n in ("xl", "xq", "a", "za", "zb", "h", "q", "yc")])
 
 
-def _engines(topo, src, dst):
+def _engines(topo, src, dst, part=None):
     full = topo.mask(src, dst)
     bits = [b for b in range(full.bit_length()) if (full >> b) & 1]
-    k = min(K_ON if topo.chip(src) == topo.chip(dst) else K_OFF, len(bits))
+    if part is not None:
+        bits = bits[part::2]
     m = 0
-    for b in bits[::len(bits) // k][:k]:
+    for b in bits:
         m |= 1 << b
-    return m, k
+    return m, len(bits)
+
+
+def _ports(T, topo, src, dst):
+    pool = [c for c in range(SIM_CORES) if topo.chip(c) == topo.chip(src) and T.rank_of(c) is None
+            and topo.may_write(c, dst)]
+    dies = sorted(set(topo.die(c) for c in pool), key=lambda d: min(c for c in pool if topo.die(c) == d))
+    return [[c for c in pool if topo.die(c) == d] for d in dies]
 
 
 def _writes(T, topo):
-    cores = list(T.cores)
-    last = cores[-1]
-    used = set()
+    c0, c1, c2, last = list(T.cores)
     out = []
 
     def hop(src, dst, j):
+        a, b = HALF[j]
         if topo.may_write(src, dst):
-            vias = [None, None]
-        else:
-            pool = [c for c in range(SIM_CORES) if topo.chip(c) == topo.chip(src) and T.rank_of(c) is None
-                    and c not in used and topo.may_write(c, dst)]
-            pool.sort(key=lambda c: topo.die(c) != topo.die(dst))
-            vias = (pool * 2)[:2]
-            used.update(vias)
-        for kind, v in enumerate(vias):
-            if v is None:
-                out.append((src, dst, kind, j, True))
-            else:
-                out.append((src, v, kind, j, True))
-                out.append((v, dst, kind, j, False))
+            out.append((src, dst, 0, j, True, a, b, None))
+            out.append((src, dst, 1, j, True, a, b, None))
+            return
+        da, db = _ports(T, topo, src, dst)[:2]
+        mid = (a + b) // 2
+        for p, (v, lo, hi) in enumerate(((da[0], a, mid), (db[0], mid, b))):
+            out.append((src, v, 0, j, True, lo, hi, p))
+            out.append((v, dst, 0, j, False, lo, hi, None))
+        v = (da[1], db[1])[j]
+        out.append((src, v, 1, j, True, a, b, None))
+        out.append((v, dst, 1, j, False, a, b, None))
 
-    for j in range(2):
-        hop(last, cores[j], j)
-        hop(cores[j], cores[2], j)
-        hop(cores[2], last, j)
+    hop(last, c0, 0)
+    hop(last, c0, 1)
+    hop(c0, c2, 0)
+    hop(c2, last, 0)
+    hop(c0, c1, 1)
+    hop(c1, last, 1)
+    return out
+
+
+def _wroutes(T, topo):
+    _c0, c1, c2, _last = list(T.cores)
+    out = []
+    for src, dst in ((c1, c2), (c2, c1)):
+        if topo.may_write(src, dst):
+            vias = [None]
+        else:
+            vias = [c for d in _ports(T, topo, src, dst) for c in d]
+        for p, (kind, i) in enumerate([(0, 0), (1, 0), (0, 1), (1, 1)]):
+            out.append((src, vias[p % len(vias)], dst, kind, i))
     return out
 
 
 def rank_program(g, core, T, topo):
     writes = _writes(T, topo)
+    wroutes = _wroutes(T, topo)
     outgoing = [w for w in writes if w[0] == core]
     incoming = [w for w in writes if w[1] == core]
-    if not outgoing and not incoming:
+    wpass = [r for r in wroutes if r[1] == core]
+    if not outgoing and not incoming and not wpass:
         return
     S = T.sem
     cores = list(T.cores)
     rank = T.rank_of(core)
     last = len(cores) - 1
-    need = [sum(_engines(topo, w[0], w[1])[1] for w in incoming if w[3] == j) for j in range(2)]
+    need = [sum(_engines(topo, w[0], w[1], w[7])[1] for w in incoming if w[3] == j) for j in range(2)]
     sent = [0]
 
     def put(dst, dst_ap, src_ap, sem):
@@ -89,21 +111,49 @@ def rank_program(g, core, T, topo):
         sent[0] += k
 
     def send(j):
-        a, b = HALF[j]
-        for (_, dst, kind, jj, fresh) in outgoing:
-            if jj != j:
-                continue
-            if kind == 0:
-                put(dst, T.icod[:, a:b].bitcast(dt.uint8), (T.ocod if fresh else T.icod)[:, a:b].bitcast(dt.uint8),
-                    S["a%d" % j])
-            else:
-                put(dst, T.iscl[:, a:b], (T.oscl if fresh else T.iscl)[:, a:b], S["a%d" % j])
+        mine = [w for w in outgoing if w[3] == j]
+        codes = [w for w in mine if w[2] == 0]
+        sem = S["a%d" % j]
+        if len(codes) > 1:
+            trs = []
+            for (_, dst, _k, _j, fresh, a, b, part) in codes:
+                rid, pid, _se = topo.addr(dst)
+                mask, k = _engines(topo, core, dst, part)
+                trs.append(RemoteDMATransfer(dst_ids=[DstId(rid=rid, pnc=pid)], dma_engine_mask=mask, remote_sem=sem,
+                                             src=(T.ocod if fresh else T.icod)[:, a:b].bitcast(dt.uint8),
+                                             dst=T.icod[:, a:b].bitcast(dt.uint8)))
+                sent[0] += k
+            g.remote_dma_fused(trs, local_sem=S.sent)
+        else:
+            for (_, dst, _k, _j, fresh, a, b, _p) in codes:
+                put(dst, T.icod[:, a:b].bitcast(dt.uint8), (T.ocod if fresh else T.icod)[:, a:b].bitcast(dt.uint8), sem)
+        for (_, dst, kind, _j, fresh, a, b, _p) in mine:
+            if kind == 1:
+                put(dst, T.iscl[:, a:b], (T.oscl if fresh else T.iscl)[:, a:b], sem)
+
+    def put_w(dst, kind, i, fresh):
+        a, b = 128 * i, 128 * i + 128
+        if kind == 0:
+            put(dst, T.vcod[:, a:b].bitcast(dt.uint8), (T.wcod if fresh else T.vcod)[:, a:b].bitcast(dt.uint8), S.wa)
+        else:
+            put(dst, T.vscl[:, a:b], (T.wscl if fresh else T.vscl)[:, a:b], S.wa)
 
     if rank is None:
+        def pass_w():
+            if wpass:
+                g.wait_ge(S.wa, sum(_engines(topo, r[0], core)[1] for r in wpass))
+                for (_, _v, dst, kind, i) in wpass:
+                    put_w(dst, kind, i, False)
+
+        x_first = any(w[0] == cores[last] for w in incoming)
+        if not x_first:
+            pass_w()
         for j in range(2):
             if need[j]:
                 g.wait_ge(S["a%d" % j], need[j])
                 send(j)
+        if x_first:
+            pass_w()
         g.wait_ge(S.sent, sent[0])
         return
 
@@ -142,35 +192,36 @@ def rank_program(g, core, T, topo):
     g.vector.wait_ge(S.wl, 16)
     g.vector.quantize_mx(T.wcod[:], T.wscl[:], T.wb[:]).then_inc(S.wq, 1)
 
-    if rank < 2:
-        other = cores[1 - rank]
-        g.wait_ge(S.wq, 1)
-        put(other, T.vcod[:].bitcast(dt.uint8), T.wcod[:].bitcast(dt.uint8), S.wa)
-        put(other, T.vscl[:], T.wscl[:], S.wa)
-        w_in = 2 * _engines(topo, other, core)[1]
-        a, b = HALF[rank]
-        for k in range(2):
-            if k == rank:
-                g.tensor.wait_ge(S.wq, 1)
-                wc, ws = T.wcod, T.wscl
-            else:
-                g.tensor.wait_ge(S.wa, w_in)
-                wc, ws = T.vcod, T.vscl
-            if k == 0:
-                g.tensor.wait_ge(S["a%d" % rank], need[rank])
-                layer(0, wc, ws, T.icod, T.iscl, a, b, T.h, T.mcod, T.mscl)
-            else:
-                g.tensor.wait_ge(S.q0, 1)
-                layer(1, wc, ws, T.mcod, T.mscl, a, b, T.h2, T.ocod, T.oscl)
-        g.wait_ge(S.q1, 1)
-        send(rank)
-    elif rank != last:
+    if rank == 0:
         g.tensor.wait_ge(S.wq, 1)
         for j, (a, b) in enumerate(HALF):
             g.tensor.wait_ge(S["a%d" % j], need[j])
             layer(j, T.wcod, T.wscl, T.icod, T.iscl, a, b, T.h, T.ocod, T.oscl)
             g.wait_ge(S["q%d" % j], 1)
             send(j)
+    elif rank != last:
+        g.wait_ge(S.wq, 1)
+        for (src, via, dst, kind, i) in wroutes:
+            if src == core:
+                put_w(dst if via is None else via, kind, i, True)
+        w_in = sum(_engines(topo, r[0] if r[1] is None else r[1], core)[1] for r in wroutes if r[2] == core)
+        j = [jj for jj in range(2) if need[jj]][0]
+        a, b = HALF[j]
+        for k in range(2):
+            if k + 1 == rank:
+                g.tensor.wait_ge(S.wq, 1)
+                wc, ws = T.wcod, T.wscl
+            else:
+                g.tensor.wait_ge(S.wa, w_in)
+                wc, ws = T.vcod, T.vscl
+            if k == 0:
+                g.tensor.wait_ge(S["a%d" % j], need[j])
+                layer(0, wc, ws, T.icod, T.iscl, a, b, T.h, T.mcod, T.mscl)
+            else:
+                g.tensor.wait_ge(S.q0, 1)
+                layer(1, wc, ws, T.mcod, T.mscl, a, b, T.h2, T.ocod, T.oscl)
+        g.wait_ge(S.q1, 1)
+        send(j)
     else:
         g.tensor.wait_ge(S.wq, 1)
         stored = 0

@@ -25,8 +25,8 @@ SCRATCH = {
     "yb": ("sbuf", [128, NT * G * NC], "float32"),
     "ps": ("psum", [128, 512 * G * 2], "float32"),
 }
-SEMAPHORES = (["wl", "wq", "wa", "yd", "sent"]
-              + [n + str(k) for k in range(2) for n in ("xl", "xq", "a", "za", "zb", "h", "q", "yc")])
+SEMAPHORES = (["wl", "wq", "wa", "ys", "sent", "hx"]
+              + [n + str(k) for k in range(2) for n in ("xl", "xq", "a", "za", "zb", "h", "q", "yc", "ye")])
 
 
 def _engines(topo, src, dst, part=None):
@@ -59,12 +59,11 @@ def _writes(T, topo):
             return
         da, db = _ports(T, topo, src, dst)[:2]
         mid = (a + b) // 2
-        for p, (v, lo, hi) in enumerate(((da[0], a, mid), (db[0], mid, b))):
-            out.append((src, v, 0, j, True, lo, hi, p))
-            out.append((v, dst, 0, j, False, lo, hi, None))
-        v = (da[1], db[1])[j]
-        out.append((src, v, 1, j, True, a, b, None))
-        out.append((v, dst, 1, j, False, a, b, None))
+        for kind in (0, 1):
+            k = j if kind == 0 else 1 - j
+            for p, (d, lo, hi) in enumerate(((da, a, mid), (db, mid, b))):
+                out.append((src, d[k], kind, j, True, lo, hi, p))
+                out.append((d[k], dst, kind, j, False, lo, hi, None))
 
     hop(last, c0, 0)
     hop(last, c0, 1)
@@ -76,7 +75,7 @@ def _writes(T, topo):
 
 
 def _wroutes(T, topo):
-    _c0, c1, c2, _last = list(T.cores)
+    c0, c1, c2, _last = list(T.cores)
     out = []
     for src, dst in ((c1, c2), (c2, c1)):
         if topo.may_write(src, dst):
@@ -84,7 +83,23 @@ def _wroutes(T, topo):
         else:
             vias = [c for d in _ports(T, topo, src, dst) for c in d]
         for p, (kind, i) in enumerate([(0, 0), (1, 0), (0, 1), (1, 1)]):
-            out.append((src, vias[p % len(vias)], dst, kind, i))
+            way = [src]
+            if kind == 1 and topo.chip(src) == topo.chip(c0):
+                way.append(c0)
+            if vias[p % len(vias)] is not None:
+                way.append(vias[p % len(vias)])
+            way.append(dst)
+            out.append((way, kind, i))
+    return out
+
+
+def _merge(runs):
+    out = []
+    for a, b in sorted(runs):
+        if out and out[-1][1] == a:
+            out[-1] = (out[-1][0], b)
+        else:
+            out.append((a, b))
     return out
 
 
@@ -93,7 +108,7 @@ def rank_program(g, core, T, topo):
     wroutes = _wroutes(T, topo)
     outgoing = [w for w in writes if w[0] == core]
     incoming = [w for w in writes if w[1] == core]
-    wpass = [r for r in wroutes if r[1] == core]
+    wpass = [r for r in wroutes if core in r[0][1:-1]]
     if not outgoing and not incoming and not wpass:
         return
     S = T.sem
@@ -110,26 +125,29 @@ def rank_program(g, core, T, topo):
                      pid=pid, routing_id=rid, dma_engine_mask=mask)
         sent[0] += k
 
+    def sides(kind, fresh, a, b):
+        if kind == 0:
+            return T.icod[:, a:b].bitcast(dt.uint8), (T.ocod if fresh else T.icod)[:, a:b].bitcast(dt.uint8)
+        return T.iscl[:, a:b], (T.oscl if fresh else T.iscl)[:, a:b]
+
     def send(j):
-        mine = [w for w in outgoing if w[3] == j]
-        codes = [w for w in mine if w[2] == 0]
         sem = S["a%d" % j]
-        if len(codes) > 1:
-            trs = []
-            for (_, dst, _k, _j, fresh, a, b, part) in codes:
-                rid, pid, _se = topo.addr(dst)
-                mask, k = _engines(topo, core, dst, part)
-                trs.append(RemoteDMATransfer(dst_ids=[DstId(rid=rid, pnc=pid)], dma_engine_mask=mask, remote_sem=sem,
-                                             src=(T.ocod if fresh else T.icod)[:, a:b].bitcast(dt.uint8),
-                                             dst=T.icod[:, a:b].bitcast(dt.uint8)))
-                sent[0] += k
-            g.remote_dma_fused(trs, local_sem=S.sent)
-        else:
-            for (_, dst, _k, _j, fresh, a, b, _p) in codes:
-                put(dst, T.icod[:, a:b].bitcast(dt.uint8), (T.ocod if fresh else T.icod)[:, a:b].bitcast(dt.uint8), sem)
-        for (_, dst, kind, _j, fresh, a, b, _p) in mine:
-            if kind == 1:
-                put(dst, T.iscl[:, a:b], (T.oscl if fresh else T.iscl)[:, a:b], sem)
+        for kind in (0, 1):
+            pieces = [w for w in outgoing if w[3] == j and w[2] == kind]
+            if len(pieces) > 1:
+                trs = []
+                for (_, dst, _k, _j, fresh, a, b, part) in pieces:
+                    rid, pid, _se = topo.addr(dst)
+                    mask, k = _engines(topo, core, dst, part)
+                    d_ap, s_ap = sides(kind, fresh, a, b)
+                    trs.append(RemoteDMATransfer(dst_ids=[DstId(rid=rid, pnc=pid)], dma_engine_mask=mask,
+                                                 remote_sem=sem, src=s_ap, dst=d_ap))
+                    sent[0] += k
+                g.remote_dma_fused(trs, local_sem=S.sent)
+            else:
+                for (_, dst, _k, _j, fresh, a, b, _p) in pieces:
+                    d_ap, s_ap = sides(kind, fresh, a, b)
+                    put(dst, d_ap, s_ap, sem)
 
     def put_w(dst, kind, i, fresh):
         a, b = 128 * i, 128 * i + 128
@@ -138,13 +156,13 @@ def rank_program(g, core, T, topo):
         else:
             put(dst, T.vscl[:, a:b], (T.wscl if fresh else T.vscl)[:, a:b], S.wa)
 
-    if rank is None:
-        def pass_w():
-            if wpass:
-                g.wait_ge(S.wa, sum(_engines(topo, r[0], core)[1] for r in wpass))
-                for (_, _v, dst, kind, i) in wpass:
-                    put_w(dst, kind, i, False)
+    def pass_w():
+        if wpass:
+            g.wait_ge(S.wa, sum(_engines(topo, way[way.index(core) - 1], core)[1] for (way, _k, _i) in wpass))
+            for (way, kind, i) in wpass:
+                put_w(way[way.index(core) + 1], kind, i, False)
 
+    if rank is None:
         x_first = any(w[0] == cores[last] for w in incoming)
         if not x_first:
             pass_w()
@@ -157,54 +175,62 @@ def rank_program(g, core, T, topo):
         g.wait_ge(S.sent, sent[0])
         return
 
-    def products(k, wc, ws, rc, rs, a, b):
-        z = []
-        for i in range(G):
-            bank = 512 * (G * k + i)
-            z.append(T.ps[:, bank:bank + b - a])
+    def products(k, wc, ws, rc, rs, a, b, order=(0, 1)):
+        z = [T.ps[:, 512 * (G * k + i):512 * (G * k + i) + b - a] for i in range(G)]
+        for i in order:
             g.tensor.matmul_mx(z[i], wc[:, 128 * i:128 * i + 128], ws[:, 128 * i:128 * i + 128],
                                rc[:, a:b], rs[:, a:b], True, True).then_inc(S[("za%d", "zb%d")[i] % k], 1)
         return z
 
-    def layer(k, wc, ws, rc, rs, a, b, hb, oc, osc):
+    def layer(k, wc, ws, rc, rs, a, b, hb, oc, osc, vector_busy=False):
         z0, z1 = products(k, wc, ws, rc, rs, a, b)
         lo, hi = 4 * a, 4 * b
         hs = S["h%d" % k]
+        relu = ActivationFunctionType.Relu
         g.scalar.wait_ge(S["za%d" % k], 1)
-        g.scalar.activation(hb[:, lo + 0:hi:4], z0, ActivationFunctionType.Relu, scale=C).then_inc(hs, 1)
-        g.scalar.activation(hb[:, lo + 1:hi:4], z0, ActivationFunctionType.Relu, scale=-C).then_inc(hs, 1)
-        g.vector.wait_ge(S["zb%d" % k], 1)
-        g.vector.tensor_scalar(hb[:, lo + 2:hi:4], z1, 0.0, C, AluOpType.max, AluOpType.mult).then_inc(hs, 1)
-        g.vector.tensor_scalar(hb[:, lo + 3:hi:4], z1, -C, 0.0, AluOpType.mult, AluOpType.max).then_inc(hs, 1)
-        g.vector.wait_ge(hs, 4)
+        if vector_busy:
+            g.scalar.activation(hb[:, lo + 0:hi:4], z0, relu, scale=C).then_inc(S.hx, 1)
+            g.scalar.wait_ge(S["zb%d" % k], 1)
+            g.scalar.activation(hb[:, lo + 2:hi:4], z1, relu, scale=C).then_inc(hs, 1)
+            g.scalar.activation(hb[:, lo + 3:hi:4], z1, relu, scale=-C).then_inc(hs, 1)
+            g.vector.wait_ge(S.hx, 1)
+            g.vector.tensor_scalar(hb[:, lo + 1:hi:4], z0, -C, 0.0, AluOpType.mult, AluOpType.max).then_inc(hs, 1)
+            g.vector.wait_ge(hs, 3)
+        else:
+            g.scalar.activation(hb[:, lo + 0:hi:4], z0, relu, scale=C).then_inc(hs, 1)
+            g.scalar.activation(hb[:, lo + 1:hi:4], z0, relu, scale=-C).then_inc(hs, 1)
+            g.vector.wait_ge(S["zb%d" % k], 1)
+            g.vector.tensor_scalar(hb[:, lo + 2:hi:4], z1, 0.0, C, AluOpType.max, AluOpType.mult).then_inc(hs, 1)
+            g.vector.tensor_scalar(hb[:, lo + 3:hi:4], z1, -C, 0.0, AluOpType.mult, AluOpType.max).then_inc(hs, 1)
+            g.vector.wait_ge(hs, 4)
         g.vector.quantize_mx(oc[:, a:b], osc[:, a:b], hb[:, lo:hi]).then_inc(S["q%d" % k], 1)
 
     if rank == last:
         for j, (a, b) in enumerate(HALF):
             g.sync.dma_start(T.xb[:, 4 * a:4 * b], T.x[:, 4 * a:4 * b]).then_inc(S["xl%d" % j], 16)
-    g.sync.dma_start(T.wb[:], T.w[:]).then_inc(S.wl, 16)
-    if rank == last:
         for j, (a, b) in enumerate(HALF):
             g.vector.wait_ge(S["xl%d" % j], 16)
             g.vector.quantize_mx(T.ocod[:, a:b], T.oscl[:, a:b], T.xb[:, 4 * a:4 * b]).then_inc(S["xq%d" % j], 1)
             g.wait_ge(S["xq%d" % j], 1)
             send(j)
+        g.sync.wait_ge(S.sent, sent[0])
+    g.sync.dma_start(T.wb[:], T.w[:]).then_inc(S.wl, 16)
     g.vector.wait_ge(S.wl, 16)
     g.vector.quantize_mx(T.wcod[:], T.wscl[:], T.wb[:]).then_inc(S.wq, 1)
 
     if rank == 0:
+        pass_w()
         g.tensor.wait_ge(S.wq, 1)
         for j, (a, b) in enumerate(HALF):
             g.tensor.wait_ge(S["a%d" % j], need[j])
-            layer(j, T.wcod, T.wscl, T.icod, T.iscl, a, b, T.h, T.ocod, T.oscl)
+            layer(j, T.wcod, T.wscl, T.icod, T.iscl, a, b, T.h, T.ocod, T.oscl, vector_busy=j > 0)
             g.wait_ge(S["q%d" % j], 1)
             send(j)
     elif rank != last:
         g.wait_ge(S.wq, 1)
-        for (src, via, dst, kind, i) in wroutes:
-            if src == core:
-                put_w(dst if via is None else via, kind, i, True)
-        w_in = sum(_engines(topo, r[0] if r[1] is None else r[1], core)[1] for r in wroutes if r[2] == core)
+        for (way, kind, i) in sorted([r for r in wroutes if r[0][0] == core], key=lambda r: -len(r[0])):
+            put_w(way[1], kind, i, True)
+        w_in = sum(_engines(topo, way[-2], core)[1] for (way, _k, _i) in wroutes if way[-1] == core)
         j = [jj for jj in range(2) if need[jj]][0]
         a, b = HALF[j]
         for k in range(2):
@@ -224,25 +250,53 @@ def rank_program(g, core, T, topo):
         send(j)
     else:
         g.tensor.wait_ge(S.wq, 1)
-        stored = 0
-        for j, (a, b) in enumerate(HALF):
-            g.tensor.wait_ge(S["a%d" % j], need[j])
-            products(j, T.wcod, T.wscl, T.icod, T.iscl, a, b)
-            g.vector.wait_ge(S["za%d" % j], 1)
-            g.scalar.wait_ge(S["zb%d" % j], 1)
-            n = 0
+        stores = [0]
+
+        def store(q, run):
+            q.dma_start(T.y[:, run[0]:run[1]], T.yb[:, run[0]:run[1]]).then_inc(S.ys, 16)
+            stores[0] += 1
+
+        def runs_of(j, i):
+            a, b = HALF[j]
+            out = []
             for m in range(a // NC, (b - 1) // NC + 1):
                 lo, hi = max(a, NC * m), min(b, NC * m + NC)
-                c0 = NC * G * m + lo - NC * m
-                p0 = 512 * G * j + lo - a
-                g.vector.tensor_copy(T.yb[:, c0:c0 + hi - lo], T.ps[:, p0:p0 + hi - lo]).then_inc(S["yc%d" % j], 1)
-                g.scalar.activation(T.yb[:, c0 + NC:c0 + NC + hi - lo], T.ps[:, p0 + 512:p0 + 512 + hi - lo],
-                                    ActivationFunctionType.Copy).then_inc(S["yc%d" % j], 1)
-                n += 2
-            g.sync.wait_ge(S["yc%d" % j], n)
-            whole = b // NC
-            g.sync.dma_start(T.y[:, NC * G * stored:NC * G * whole],
-                             T.yb[:, NC * G * stored:NC * G * whole]).then_inc(S.yd, 16)
-            stored = whole
-        g.sync.wait_ge(S.yd, 16 * len(HALF))
+                out.append((NC * (G * m + i) + lo - NC * m, 512 * (G * j + i) + lo - a, hi - lo))
+            return out
+
+        held = []
+        for j, (a, b) in enumerate(HALF):
+            end = j + 1 == len(HALF)
+            g.tensor.wait_ge(S["a%d" % j], need[j])
+            products(j, T.wcod, T.wscl, T.icod, T.iscl, a, b, (1, 0) if end else (0, 1))
+            runs = [[], []]
+            for i in range(G):
+                (g.vector, g.scalar)[i].wait_ge(S[("za%d", "zb%d")[i] % j], 1)
+                for (c0, p0, n) in runs_of(j, i):
+                    if i == 0:
+                        g.vector.tensor_copy(T.yb[:, c0:c0 + n], T.ps[:, p0:p0 + n]).then_inc(S["yc%d" % j], 1)
+                    else:
+                        g.scalar.activation(T.yb[:, c0:c0 + n], T.ps[:, p0:p0 + n],
+                                            ActivationFunctionType.Copy).then_inc(S["ye%d" % j], 1)
+                    runs[i].append((c0, c0 + n))
+            if not end:
+                later = [(c0, c0 + n) for jj in range(j + 1, len(HALF)) for i in range(G)
+                         for (c0, _p, n) in runs_of(jj, i)]
+                g.sync.wait_ge(S["yc%d" % j], len(runs[0]))
+                g.sync.wait_ge(S["ye%d" % j], len(runs[1]))
+                for run in _merge(held + runs[0] + runs[1]):
+                    if any(r[1] == run[0] for r in later) and any(r[0] == run[1] for r in later):
+                        held.append(run)
+                    else:
+                        store(g.sync, run)
+            else:
+                early = [r for r in runs[1] if not any(q[0] == r[1] for q in runs[0])]
+                g.scalar.wait_ge(S["ye%d" % j], len(runs[1]))
+                for run in early:
+                    store(g.scalar, run)
+                g.sync.wait_ge(S["ye%d" % j], len(runs[1]))
+                g.sync.wait_ge(S["yc%d" % j], len(runs[0]))
+                for run in _merge(held + runs[0] + [r for r in runs[1] if r not in early]):
+                    store(g.sync, run)
+        g.sync.wait_ge(S.ys, 16 * stores[0])
     g.wait_ge(S.sent, sent[0])

from concourse.bass import DstId, RemoteDMATransfer
from concourse.mybir import dt, AluOpType, ActivationFunctionType

SIM_CORES = 96
NT, NC, G = 3, 128, 2
NW = NT * NC
C = 0.037
HALF = [(0, NW // 2), (NW // 2, NW)]

SCRATCH = {
    "xb": ("sbuf", [128, 4 * NW], "bfloat16"),
    "wb": ("sbuf", [128, G * 512], "bfloat16"),
    "wcod": ("sbuf", [128, G * 128], "float8_e4m3fn_x4"),
    "wscl": ("sbuf", [128, G * 128], "uint8"),
    "vcod": ("sbuf", [128, G * 128], "float8_e4m3fn_x4"),
    "vscl": ("sbuf", [128, G * 128], "uint8"),
    "icod": ("sbuf", [128, NW], "float8_e4m3fn_x4"),
    "iscl": ("sbuf", [128, NW], "uint8"),
    "mcod": ("sbuf", [128, NW], "float8_e4m3fn_x4"),
    "mscl": ("sbuf", [128, NW], "uint8"),
    "ocod": ("sbuf", [128, NW], "float8_e4m3fn_x4"),
    "oscl": ("sbuf", [128, NW], "uint8"),
    "h": ("sbuf", [128, 4 * NW], "bfloat16"),
    "h2": ("sbuf", [128, 4 * NW], "bfloat16"),
    "yb": ("sbuf", [128, NT * G * NC], "float32"),
    "ps": ("psum", [128, 512 * G * 2], "float32"),
}
SEMAPHORES = (["wl", "wq", "wa", "ys", "sent", "hx"]
              + [n + str(k) for k in range(2) for n in ("xl", "xq", "a", "za", "zb", "h", "q", "yc", "ye")])


def _engines(topo, src, dst, part=None):
    full = topo.mask(src, dst)
    bits = [b for b in range(full.bit_length()) if (full >> b) & 1]
    if part is not None:
        bits = bits[part::2]
    m = 0
    for b in bits:
        m |= 1 << b
    return m, len(bits)


def _ports(T, topo, src, dst):
    pool = [c for c in range(SIM_CORES) if topo.chip(c) == topo.chip(src) and T.rank_of(c) is None
            and topo.may_write(c, dst)]
    dies = sorted(set(topo.die(c) for c in pool), key=lambda d: min(c for c in pool if topo.die(c) == d))
    return [[c for c in pool if topo.die(c) == d] for d in dies]


def _writes(T, topo):
    c0, c1, c2, last = list(T.cores)
    out = []

    def hop(src, dst, j):
        a, b = HALF[j]
        if topo.may_write(src, dst):
            out.append((src, dst, 0, j, True, a, b, None))
            out.append((src, dst, 1, j, True, a, b, None))
            return
        da, db = _ports(T, topo, src, dst)[:2]
        mid = (a + b) // 2
        for kind in (0, 1):
            k = j if kind == 0 else 1 - j
            for p, (d, lo, hi) in enumerate(((da, a, mid), (db, mid, b))):
                out.append((src, d[k], kind, j, True, lo, hi, p))
                out.append((d[k], dst, kind, j, False, lo, hi, None))

    hop(last, c0, 0)
    hop(last, c0, 1)
    hop(c0, c2, 0)
    hop(c2, last, 0)
    hop(c0, c1, 1)
    hop(c1, last, 1)
    return out


def _wroutes(T, topo):
    c0, c1, c2, _last = list(T.cores)
    out = []
    for src, dst in ((c1, c2), (c2, c1)):
        if topo.may_write(src, dst):
            vias = [None]
        else:
            vias = [c for d in _ports(T, topo, src, dst) for c in d]
        for p, (kind, i) in enumerate([(0, 0), (1, 0), (0, 1), (1, 1)]):
            way = [src]
            if kind == 1 and topo.chip(src) == topo.chip(c0):
                way.append(c0)
            if vias[p % len(vias)] is not None:
                way.append(vias[p % len(vias)])
            way.append(dst)
            out.append((way, kind, i))
    return out


def _merge(runs):
    out = []
    for a, b in sorted(runs):
        if out and out[-1][1] == a:
            out[-1] = (out[-1][0], b)
        else:
            out.append((a, b))
    return out


def rank_program(g, core, T, topo):
    writes = _writes(T, topo)
    wroutes = _wroutes(T, topo)
    outgoing = [w for w in writes if w[0] == core]
    incoming = [w for w in writes if w[1] == core]
    wpass = [r for r in wroutes if core in r[0][1:-1]]
    if not outgoing and not incoming and not wpass:
        return
    S = T.sem
    cores = list(T.cores)
    rank = T.rank_of(core)
    last = len(cores) - 1
    need = [sum(_engines(topo, w[0], w[1], w[7])[1] for w in incoming if w[3] == j) for j in range(2)]
    sent = [0]

    def put(dst, dst_ap, src_ap, sem):
        rid, pid, _se = topo.addr(dst)
        mask, k = _engines(topo, core, dst)
        g.remote_dma(out_ap=dst_ap, in_ap=src_ap, remote_sem=sem, local_sem=S.sent,
                     pid=pid, routing_id=rid, dma_engine_mask=mask)
        sent[0] += k

    def sides(kind, fresh, a, b):
        if kind == 0:
            return T.icod[:, a:b].bitcast(dt.uint8), (T.ocod if fresh else T.icod)[:, a:b].bitcast(dt.uint8)
        return T.iscl[:, a:b], (T.oscl if fresh else T.iscl)[:, a:b]

    def send(j):
        sem = S["a%d" % j]
        for kind in (0, 1):
            pieces = [w for w in outgoing if w[3] == j and w[2] == kind]
            if len(pieces) > 1:
                trs = []
                for (_, dst, _k, _j, fresh, a, b, part) in pieces:
                    rid, pid, _se = topo.addr(dst)
                    mask, k = _engines(topo, core, dst, part)
                    d_ap, s_ap = sides(kind, fresh, a, b)
                    trs.append(RemoteDMATransfer(dst_ids=[DstId(rid=rid, pnc=pid)], dma_engine_mask=mask,
                                                 remote_sem=sem, src=s_ap, dst=d_ap))
                    sent[0] += k
                g.remote_dma_fused(trs, local_sem=S.sent)
            else:
                for (_, dst, _k, _j, fresh, a, b, _p) in pieces:
                    d_ap, s_ap = sides(kind, fresh, a, b)
                    put(dst, d_ap, s_ap, sem)

    def put_w(dst, kind, i, fresh):
        a, b = 128 * i, 128 * i + 128
        if kind == 0:
            put(dst, T.vcod[:, a:b].bitcast(dt.uint8), (T.wcod if fresh else T.vcod)[:, a:b].bitcast(dt.uint8), S.wa)
        else:
            put(dst, T.vscl[:, a:b], (T.wscl if fresh else T.vscl)[:, a:b], S.wa)

    def pass_w():
        if wpass:
            g.wait_ge(S.wa, sum(_engines(topo, way[way.index(core) - 1], core)[1] for (way, _k, _i) in wpass))
            for (way, kind, i) in wpass:
                put_w(way[way.index(core) + 1], kind, i, False)

    if rank is None:
        x_first = any(w[0] == cores[last] for w in incoming)
        if not x_first:
            pass_w()
        for j in range(2):
            if need[j]:
                g.wait_ge(S["a%d" % j], need[j])
                send(j)
        if x_first:
            pass_w()
        g.wait_ge(S.sent, sent[0])
        return

    def products(k, wc, ws, rc, rs, a, b, order=(0, 1)):
        z = [T.ps[:, 512 * (G * k + i):512 * (G * k + i) + b - a] for i in range(G)]
        for i in order:
            g.tensor.matmul_mx(z[i], wc[:, 128 * i:128 * i + 128], ws[:, 128 * i:128 * i + 128],
                               rc[:, a:b], rs[:, a:b], True, True).then_inc(S[("za%d", "zb%d")[i] % k], 1)
        return z

    def layer(k, wc, ws, rc, rs, a, b, hb, oc, osc, vector_busy=False):
        z0, z1 = products(k, wc, ws, rc, rs, a, b)
        lo, hi = 4 * a, 4 * b
        hs = S["h%d" % k]
        relu = ActivationFunctionType.Relu
        g.scalar.wait_ge(S["za%d" % k], 1)
        if vector_busy:
            g.scalar.activation(hb[:, lo + 0:hi:4], z0, relu, scale=C).then_inc(S.hx, 1)
            g.scalar.wait_ge(S["zb%d" % k], 1)
            g.scalar.activation(hb[:, lo + 2:hi:4], z1, relu, scale=C).then_inc(hs, 1)
            g.scalar.activation(hb[:, lo + 3:hi:4], z1, relu, scale=-C).then_inc(hs, 1)
            g.vector.wait_ge(S.hx, 1)
            g.vector.tensor_scalar(hb[:, lo + 1:hi:4], z0, -C, 0.0, AluOpType.mult, AluOpType.max).then_inc(hs, 1)
            g.vector.wait_ge(hs, 3)
        else:
            g.scalar.activation(hb[:, lo + 0:hi:4], z0, relu, scale=C).then_inc(hs, 1)
            g.scalar.activation(hb[:, lo + 1:hi:4], z0, relu, scale=-C).then_inc(hs, 1)
            g.vector.wait_ge(S["zb%d" % k], 1)
            g.vector.tensor_scalar(hb[:, lo + 2:hi:4], z1, 0.0, C, AluOpType.max, AluOpType.mult).then_inc(hs, 1)
            g.vector.tensor_scalar(hb[:, lo + 3:hi:4], z1, -C, 0.0, AluOpType.mult, AluOpType.max).then_inc(hs, 1)
            g.vector.wait_ge(hs, 4)
        g.vector.quantize_mx(oc[:, a:b], osc[:, a:b], hb[:, lo:hi]).then_inc(S["q%d" % k], 1)

    if rank == last:
        for j, (a, b) in enumerate(HALF):
            g.sync.dma_start(T.xb[:, 4 * a:4 * b], T.x[:, 4 * a:4 * b]).then_inc(S["xl%d" % j], 16)
        for j, (a, b) in enumerate(HALF):
            g.vector.wait_ge(S["xl%d" % j], 16)
            g.vector.quantize_mx(T.ocod[:, a:b], T.oscl[:, a:b], T.xb[:, 4 * a:4 * b]).then_inc(S["xq%d" % j], 1)
            g.wait_ge(S["xq%d" % j], 1)
            send(j)
        g.sync.wait_ge(S.sent, sent[0])
    g.sync.dma_start(T.wb[:], T.w[:]).then_inc(S.wl, 16)
    g.vector.wait_ge(S.wl, 16)
    g.vector.quantize_mx(T.wcod[:], T.wscl[:], T.wb[:]).then_inc(S.wq, 1)

    if rank == 0:
        pass_w()
        g.tensor.wait_ge(S.wq, 1)
        for j, (a, b) in enumerate(HALF):
            g.tensor.wait_ge(S["a%d" % j], need[j])
            layer(j, T.wcod, T.wscl, T.icod, T.iscl, a, b, T.h, T.ocod, T.oscl, vector_busy=j > 0)
            g.wait_ge(S["q%d" % j], 1)
            send(j)
    elif rank != last:
        g.wait_ge(S.wq, 1)
        for (way, kind, i) in sorted([r for r in wroutes if r[0][0] == core], key=lambda r: -len(r[0])):
            put_w(way[1], kind, i, True)
        w_in = sum(_engines(topo, way[-2], core)[1] for (way, _k, _i) in wroutes if way[-1] == core)
        j = [jj for jj in range(2) if need[jj]][0]
        a, b = HALF[j]
        for k in range(2):
            if k + 1 == rank:
                g.tensor.wait_ge(S.wq, 1)
                wc, ws = T.wcod, T.wscl
            else:
                g.tensor.wait_ge(S.wa, w_in)
                wc, ws = T.vcod, T.vscl
            if k == 0:
                g.tensor.wait_ge(S["a%d" % j], need[j])
                layer(0, wc, ws, T.icod, T.iscl, a, b, T.h, T.mcod, T.mscl)
            else:
                g.tensor.wait_ge(S.q0, 1)
                layer(1, wc, ws, T.mcod, T.mscl, a, b, T.h2, T.ocod, T.oscl)
        g.wait_ge(S.q1, 1)
        send(j)
    else:
        g.tensor.wait_ge(S.wq, 1)
        stores = [0]

        def store(q, run):
            q.dma_start(T.y[:, run[0]:run[1]], T.yb[:, run[0]:run[1]]).then_inc(S.ys, 16)
            stores[0] += 1

        def runs_of(j, i):
            a, b = HALF[j]
            out = []
            for m in range(a // NC, (b - 1) // NC + 1):
                lo, hi = max(a, NC * m), min(b, NC * m + NC)
                out.append((NC * (G * m + i) + lo - NC * m, 512 * (G * j + i) + lo - a, hi - lo))
            return out

        held = []
        for j, (a, b) in enumerate(HALF):
            end = j + 1 == len(HALF)
            g.tensor.wait_ge(S["a%d" % j], need[j])
            products(j, T.wcod, T.wscl, T.icod, T.iscl, a, b, (1, 0) if end else (0, 1))
            runs = [[], []]
            for i in range(G):
                (g.vector, g.scalar)[i].wait_ge(S[("za%d", "zb%d")[i] % j], 1)
                for (c0, p0, n) in runs_of(j, i):
                    if i == 0:
                        g.vector.tensor_copy(T.yb[:, c0:c0 + n], T.ps[:, p0:p0 + n]).then_inc(S["yc%d" % j], 1)
                    else:
                        g.scalar.activation(T.yb[:, c0:c0 + n], T.ps[:, p0:p0 + n],
                                            ActivationFunctionType.Copy).then_inc(S["ye%d" % j], 1)
                    runs[i].append((c0, c0 + n))
            if not end:
                later = [(c0, c0 + n) for jj in range(j + 1, len(HALF)) for i in range(G)
                         for (c0, _p, n) in runs_of(jj, i)]
                g.sync.wait_ge(S["yc%d" % j], len(runs[0]))
                g.sync.wait_ge(S["ye%d" % j], len(runs[1]))
                for run in _merge(held + runs[0] + runs[1]):
                    if any(r[1] == run[0] for r in later) and any(r[0] == run[1] for r in later):
                        held.append(run)
                    else:
                        store(g.sync, run)
            else:
                early = [r for r in runs[1] if not any(q[0] == r[1] for q in runs[0])]
                g.scalar.wait_ge(S["ye%d" % j], len(runs[1]))
                for run in early:
                    store(g.scalar, run)
                g.sync.wait_ge(S["ye%d" % j], len(runs[1]))
                g.sync.wait_ge(S["yc%d" % j], len(runs[0]))
                for run in _merge(held + runs[0] + [r for r in runs[1] if r not in early]):
                    store(g.sync, run)
        g.sync.wait_ge(S.ys, 16 * stores[0])
    g.wait_ge(S.sent, sent[0])
